import numpy as np
import ml_dtypes


def mxq(x, axis, fmt="e4m3"):
    dtype, down = {"e4m3": (ml_dtypes.float8_e4m3fn, 7), "e5m2": (ml_dtypes.float8_e5m2, 14)}[fmt]
    v = np.moveaxis(np.asarray(x, np.float32).astype(ml_dtypes.bfloat16).astype(np.float64), axis, -1)
    blocks = v.reshape(v.shape[:-1] + (-1, 32))
    amax = np.abs(blocks).max(-1, keepdims=True)
    byte = np.maximum(np.where(amax > 0, np.frexp(amax)[1] - 1 + 127, 0) - down, 1)
    scale = np.exp2(byte - 127.0)
    codes = (blocks / scale).astype(np.float32).astype(dtype).astype(np.float64)
    return np.moveaxis((codes * scale).reshape(v.shape), -1, axis)


WIDE = False


def mx_kscale(k):
    if not WIDE:
        return np.ones(k)
    levels = np.array([10, -10, 5, -5, 0])
    if k % 512:
        return np.exp2(np.random.permutation(np.resize(levels, k // 32))).repeat(32)
    a = np.empty((k // 512, 16))
    for p in range(k // 512):
        a[p, :8] = np.random.permutation(np.resize(levels, 8))
        for g in range(8):
            far = levels[np.abs(levels - a[p, g]) >= 10]
            a[p, g + 8] = far[np.random.randint(len(far))]
    return np.exp2(a.ravel()).repeat(32)


def f64(x):
    return np.asarray(x).astype(np.float64)


def striped8(idx):
    return np.asarray(idx).reshape(8, -1, 16).transpose(0, 2, 1).reshape(128, -1).astype(np.uint16)


def unstriped8(offs):
    return offs.reshape(8, 16, -1).transpose(0, 2, 1).reshape(8, -1).astype(np.int64)


def pick8(x, idx, run):
    r = np.arange(len(x))
    return x[r[:, None], idx[r % (8 * run) // run]]


E2M1 = np.array([0.0, 0.5, 1.0, 1.5, 2.0, 3.0, 4.0, 6.0, -0.0, -0.5, -1.0, -1.5, -2.0, -3.0, -4.0, -6.0])


def pack_weight(w, fmt):
    k, n = w.shape
    w = f64(np.asarray(w, np.float32).astype(ml_dtypes.bfloat16)).reshape(k // 32, 32, n)
    amax = np.abs(w).max(1)
    if fmt == "e4m3":
        byte = np.frexp(amax)[1] - 1 + 127 - 7
    else:
        mant, ex = np.frexp(amax / 6.0)
        byte = np.where(mant > 0.5, ex, ex - 1) + 127
    byte = np.clip(np.where(amax > 0, byte, 1), 1, 254)
    scaled = (w * np.exp2(127.0 - byte)[:, None, :]).reshape(k, n).astype(np.float32)
    by_word = np.ascontiguousarray(scaled.reshape(k // 512, 128, 4, n).transpose(0, 1, 3, 2))
    if fmt == "e4m3":
        words = by_word.astype(ml_dtypes.float8_e4m3fn).view(np.uint8)
    else:
        c = by_word.astype(ml_dtypes.float4_e2m1fn).view(np.uint8) & 0xF
        words = (c[..., 0::2] | (c[..., 1::2] << 4)).reshape(k // 512, 128, 2 * n)
    return np.ascontiguousarray(words), np.ascontiguousarray(byte.astype(np.uint8).reshape(k // 512, 16, n))


def unpack_weight(words, scales, fmt):
    g, _, n = scales.shape
    words = np.ascontiguousarray(words).reshape(g, 128, n, -1)
    if fmt == "e4m3":
        vals = words.view(ml_dtypes.float8_e4m3fn).astype(np.float64)
    else:
        nib = np.empty((g, 128, n, 4), np.uint8)
        nib[..., 0::2] = words & 0xF
        nib[..., 1::2] = words >> 4
        vals = E2M1[nib]
    vals = vals * np.repeat(np.exp2(scales.astype(np.float64) - 127.0), 8, axis=1)[..., None]
    return vals.transpose(0, 1, 3, 2).reshape(g * 512, n)


def sgn(shape):
    return np.random.uniform(0.5, 2.0, shape) * np.where(np.random.standard_normal(shape) < 0, -1.0, 1.0)


D, T, U, I, Q = 512, 1024, 1024, 512, 128


def setup_inputs():
    n = np.random.standard_normal
    idx = np.stack([np.random.permutation(T)[:I] for _ in range(8)])
    idx2 = np.stack([np.random.permutation(U)[:I] for _ in range(8)])
    idx3 = np.stack([np.random.permutation(U)[:I] for _ in range(8)])
    idx4 = np.stack([np.random.permutation(T)[:I] for _ in range(8)])
    idx5 = np.stack([np.random.permutation(T)[:I] for _ in range(8)])
    fd = mx_kscale(D)
    cachep = pack_weight(n((D, T)) / fd[:, None], "e4m3")
    draftp = pack_weight(n((D, U)) / fd[:, None], "e2m1")
    return {
        "query": (n((D, Q)) * 1.0 / np.sqrt(D) * fd[:, None]).astype(np.float32),
        "cache_words": cachep[0],
        "cache_scales": cachep[1],
        "draft_words": draftp[0],
        "draft_scales": draftp[1],
        "sa": (sgn((Q, 1))).astype(np.float32),
        "sb": (sgn((Q, 1))).astype(np.float32),
        "offs": striped8(idx),
        "offs2": striped8(idx2),
        "offs3": striped8(idx3),
        "offs4": striped8(idx4),
        "offs5": striped8(idx5),
    }


def reference(query, cache_words, cache_scales, draft_words, draft_scales, sa, sb, offs, offs2, offs3, offs4, offs5):
    idx = unstriped8(offs)
    idx2 = unstriped8(offs2)
    idx3 = unstriped8(offs3)
    idx4 = unstriped8(offs4)
    idx5 = unstriped8(offs5)
    cacheu = unpack_weight(cache_words, cache_scales, "e4m3")
    draftu = unpack_weight(draft_words, draft_scales, "e2m1")
    queryq = mxq(f64(query), 0, "e4m3")
    a = queryq.T @ cacheu
    b = queryq.T @ draftu
    f1 = np.zeros((Q, U))
    f1[np.arange(Q)[:, None], idx2[np.arange(Q) % 128 // 16]] = pick8(a, idx, 16)
    bb = b + f1
    w = pick8(bb, idx3, 16) * f64(sb)
    f2 = np.zeros((Q, T))
    f2[np.arange(Q)[:, None], idx4[np.arange(Q) % 128 // 16]] = w
    aa = a - f2
    v = pick8(aa, idx5, 16) * f64(sa)
    y = v - w
    return y

@@ -1,0 +1,146 @@
+from contextlib import ExitStack
+
+import concourse.mybir as mybir
+
+D, T, U, I, Q = 512, 1024, 1024, 512, 128
+FLOPS = 2 * D * Q * (T + U)
+
+F32 = mybir.dt.float32
+BF16 = mybir.dt.bfloat16
+I32 = mybir.dt.int32
+U32 = mybir.dt.uint32
+U16 = mybir.dt.uint16
+U8 = mybir.dt.uint8
+FP8X4 = mybir.dt.float8_e4m3fn_x4
+FP4X4 = mybir.dt.float4_e2m1fn_x4
+COPY = mybir.ActivationFunctionType.Copy
+ADD = mybir.AluOpType.add
+SUB = mybir.AluOpType.subtract
+
+P = 128
+PACK = 4
+A_COLS = 256
+B_COLS = 512
+HALF = I // 2
+LIST_COLS = I // 16
+
+
+def tile_attend_scaledreturn_two_kernel(
+    tc, query, cache_words, cache_scales, draft_words, draft_scales, sa, sb, offs, offs2, offs3, offs4, offs5, out
+):
+    nc = tc.nc
+    with ExitStack() as ctx:
+        keep = ctx.enter_context(tc.tile_pool(name="keep", bufs=1))
+        psum = ctx.enter_context(tc.psum_pool(name="psum", bufs=1))
+
+        def load_list(src, name):
+            tile = keep.tile([P, LIST_COLS], U16, name=name)
+            nc.sync.dma_start(tile[:], src)
+            return tile
+
+        def load_scales(engine, src, name):
+            plane = keep.tile([P, T], U8, name=name, align_bytes=64)
+            for quad in range(4):
+                engine.dma_start(
+                    plane[32 * quad : 32 * quad + 4, :].bitcast(I32),
+                    src[0, 4 * quad : 4 * quad + 4, :].bitcast(I32),
+                )
+            return plane
+
+        q_raw = keep.tile([P, PACK, Q], F32, name="q_raw")
+        nc.sync.dma_start(q_raw[:], query.rearrange("(p j) q -> p j q", j=PACK))
+        c_scales = load_scales(nc.scalar, cache_scales, "c_scales")
+        c_flat = cache_words[0].rearrange("p n t -> p (n t)")
+        c_words = []
+        for h in range(2):
+            tile = keep.tile([P, T // 2], I32, name=f"c_words{h}", align_bytes=64)
+            nc.sync.dma_start(tile[:], c_flat[:, h * 2 * T : (h + 1) * 2 * T].bitcast(I32))
+            c_words.append(tile)
+        l1 = load_list(offs, "l1")
+        l2 = load_list(offs2, "l2")
+        d_words = keep.tile([P, 2 * U], U8, name="d_words", align_bytes=64)
+        nc.sync.dma_start(d_words[:].bitcast(I32), draft_words[0].bitcast(I32))
+        d_scales = load_scales(nc.sync, draft_scales, "d_scales")
+        l3 = load_list(offs3, "l3")
+        sb_col = keep.tile([P, 1], F32, name="sb_col")
+        nc.sync.dma_start(sb_col[:], sb)
+        l4 = load_list(offs4, "l4")
+        l5 = load_list(offs5, "l5")
+        sa_col = keep.tile([P, 1], F32, name="sa_col")
+        nc.sync.dma_start(sa_col[:], sa)
+
+        f1 = keep.tile([P, U], F32, name="f1")
+        f2 = keep.tile([P, T], F32, name="f2")
+        nc.vector.memset(f1[:], 0.0)
+        nc.vector.memset(f2[:], 0.0)
+
+        q_bf = keep.tile([P, Q, PACK], BF16, name="q_bf", align_bytes=64)
+        nc.vector.tensor_copy(
+            out=q_bf[:].rearrange("p (c i) t -> p c t i", i=4),
+            in_=q_raw[:].rearrange("p t (c i) -> p c t i", i=4),
+        )
+        q_words = keep.tile([P, Q], U32, name="q_words", align_bytes=64)
+        q_scales = keep.tile([P, Q], U8, name="q_scales", align_bytes=64)
+        nc.vector.quantize_mx(
+            out=q_words[:].bitcast(FP8X4), scales=q_scales[:], in_=q_bf[:].rearrange("p q t -> p (q t)")
+        )
+
+        a_sb = keep.tile([P, T], F32, name="a_sb")
+        for c in range(T // A_COLS):
+            bank = psum.tile([P, A_COLS], F32, name=f"a_bank{c}")
+            cols = slice(c * A_COLS, (c + 1) * A_COLS)
+            h, c0 = divmod(c * A_COLS, T // 2)
+            nc.tensor.matmul_mx(
+                out=bank[:],
+                lhsT=q_words[:].bitcast(FP8X4),
+                lhsT_scale=q_scales[:],
+                rhs=c_words[h][:, c0 : c0 + A_COLS].bitcast(FP8X4),
+                rhs_scale=c_scales[:, cols],
+                start=True,
+                stop=True,
+            )
+            if c % 2 == 0:
+                nc.scalar.copy(a_sb[:, cols], bank[:])
+            else:
+                nc.vector.tensor_copy(out=a_sb[:, cols], in_=bank[:])
+
+        b_banks = []
+        for c in range(U // B_COLS):
+            bank = psum.tile([P, B_COLS], F32, name=f"b_bank{c}")
+            nc.tensor.matmul_mx(
+                out=bank[:],
+                lhsT=q_words[:].bitcast(FP8X4),
+                lhsT_scale=q_scales[:],
+                rhs=d_words[:, 2 * c * B_COLS : 2 * (c + 1) * B_COLS].bitcast(FP4X4),
+                rhs_scale=d_scales[:, c * B_COLS : (c + 1) * B_COLS],
+                start=True,
+                stop=True,
+            )
+            b_banks.append(bank)
+
+        for h in range(2):
+            part = slice(h * LIST_COLS // 2, (h + 1) * LIST_COLS // 2)
+            picked = keep.tile([P, HALF], F32, name=f"picked{h}")
+            nc.vector.tensor_copy(picked[:], a_sb[:].indirect(l1[:, part]))
+            nc.scalar.activation(f1[:].indirect(l2[:, part]), picked[:], COPY)
+
+        bb = keep.tile([P, U], F32, name="bb")
+        for c in range(U // B_COLS):
+            cols = slice(c * B_COLS, (c + 1) * B_COLS)
+            nc.vector.tensor_tensor(bb[:, cols], b_banks[c][:], f1[:, cols], ADD)
+
+        w = keep.tile([P, I], F32, name="w")
+        nc.scalar.activation(w[:], bb[:].indirect(l3[:]), COPY, scale=sb_col[:])
+        nc.scalar.activation(f2[:].indirect(l4[:]), w[:], COPY)
+
+        aa = keep.tile([P, T], F32, name="aa")
+        nc.vector.tensor_tensor(aa[:], a_sb[:], f2[:], SUB)
+
+        for h in range(2):
+            part = slice(h * LIST_COLS // 2, (h + 1) * LIST_COLS // 2)
+            cols = slice(h * HALF, (h + 1) * HALF)
+            v = keep.tile([P, HALF], F32, name=f"v{h}")
+            nc.scalar.activation(v[:], aa[:].indirect(l5[:, part]), COPY, scale=sa_col[:])
+            y = keep.tile([P, HALF], F32, name=f"y{h}")
+            nc.vector.tensor_tensor(y[:], v[:], w[:, cols], SUB)
+            nc.sync.dma_start(out[:, cols], y[:])

@@ -19,7 +19,9 @@ SUB = mybir.AluOpType.subtract
 
 P = 128
 PACK = 4
-A_COLS = 256
+A_PIECES = (512, 256, 128, 128)
+SPLIT = 704
+C_LOADS = ((0, 512), (512, 768), (768, 1024))
 B_COLS = 512
 HALF = I // 2
 LIST_COLS = I // 16
@@ -49,12 +51,12 @@ def tile_attend_scaledreturn_two_kernel(
 
         q_raw = keep.tile([P, PACK, Q], F32, name="q_raw")
         nc.sync.dma_start(q_raw[:], query.rearrange("(p j) q -> p j q", j=PACK))
-        c_scales = load_scales(nc.scalar, cache_scales, "c_scales")
+        c_scales = load_scales(nc.sync, cache_scales, "c_scales")
         c_flat = cache_words[0].rearrange("p n t -> p (n t)")
         c_words = []
-        for h in range(2):
-            tile = keep.tile([P, T // 2], I32, name=f"c_words{h}", align_bytes=64)
-            nc.sync.dma_start(tile[:], c_flat[:, h * 2 * T : (h + 1) * 2 * T].bitcast(I32))
+        for c0, c1 in C_LOADS:
+            tile = keep.tile([P, c1 - c0], I32, name=f"c_words{c0}", align_bytes=64)
+            nc.sync.dma_start(tile[:], c_flat[:, PACK * c0 : PACK * c1].bitcast(I32))
             c_words.append(tile)
         l1 = load_list(offs, "l1")
         l2 = load_list(offs2, "l2")
@@ -86,23 +88,28 @@ def tile_attend_scaledreturn_two_kernel(
         )
 
         a_sb = keep.tile([P, T], F32, name="a_sb")
-        for c in range(T // A_COLS):
-            bank = psum.tile([P, A_COLS], F32, name=f"a_bank{c}")
-            cols = slice(c * A_COLS, (c + 1) * A_COLS)
-            h, c0 = divmod(c * A_COLS, T // 2)
+        a_banks = []
+        start = 0
+        for c, width in enumerate(A_PIECES):
+            bank = psum.tile([P, width], F32, name=f"a_bank{c}")
+            cols = slice(start, start + width)
+            h = max(n for n, load in enumerate(C_LOADS) if load[0] <= start)
+            c0 = start - C_LOADS[h][0]
             nc.tensor.matmul_mx(
                 out=bank[:],
                 lhsT=q_words[:].bitcast(FP8X4),
                 lhsT_scale=q_scales[:],
-                rhs=c_words[h][:, c0 : c0 + A_COLS].bitcast(FP8X4),
+                rhs=c_words[h][:, c0 : c0 + width].bitcast(FP8X4),
                 rhs_scale=c_scales[:, cols],
                 start=True,
                 stop=True,
             )
-            if c % 2 == 0:
+            if c in (0, 3):
                 nc.scalar.copy(a_sb[:, cols], bank[:])
             else:
                 nc.vector.tensor_copy(out=a_sb[:, cols], in_=bank[:])
+            a_banks.append(bank)
+            start = start + width
 
         b_banks = []
         for c in range(U // B_COLS):
@@ -118,11 +125,10 @@ def tile_attend_scaledreturn_two_kernel(
             )
             b_banks.append(bank)
 
-        for h in range(2):
-            part = slice(h * LIST_COLS // 2, (h + 1) * LIST_COLS // 2)
-            picked = keep.tile([P, HALF], F32, name=f"picked{h}")
-            nc.vector.tensor_copy(picked[:], a_sb[:].indirect(l1[:, part]))
-            nc.scalar.activation(f1[:].indirect(l2[:, part]), picked[:], COPY)
+        picked = keep.tile([P, I], F32, name="picked")
+        nc.scalar.activation(picked[:, :HALF], a_sb[:].indirect(l1[:, : LIST_COLS // 2]), COPY)
+        nc.vector.tensor_copy(picked[:, HALF:], a_sb[:].indirect(l1[:, LIST_COLS // 2 :]))
+        nc.scalar.activation(f1[:].indirect(l2[:]), picked[:], COPY)
 
         bb = keep.tile([P, U], F32, name="bb")
         for c in range(U // B_COLS):

@@ -20,7 +20,8 @@ SUB = mybir.AluOpType.subtract
 P = 128
 PACK = 4
 A_PIECES = (512, 256, 128, 128)
-SPLIT = 704
+SHARE = 352
+SPLIT = T - SHARE
 C_LOADS = ((0, 512), (512, 768), (768, 1024))
 B_COLS = 512
 HALF = I // 2
@@ -130,17 +131,21 @@ def tile_attend_scaledreturn_two_kernel(
         nc.vector.tensor_copy(picked[:, HALF:], a_sb[:].indirect(l1[:, LIST_COLS // 2 :]))
         nc.scalar.activation(f1[:].indirect(l2[:]), picked[:], COPY)
 
+        b_head = a_sb[:, :SHARE]
+        nc.vector.tensor_copy(out=b_head, in_=b_banks[0][:, :SHARE])
         bb = keep.tile([P, U], F32, name="bb")
-        for c in range(U // B_COLS):
-            cols = slice(c * B_COLS, (c + 1) * B_COLS)
-            nc.vector.tensor_tensor(bb[:, cols], b_banks[c][:], f1[:, cols], ADD)
+        nc.gpsimd.tensor_tensor(bb[:, :SHARE], b_head, f1[:, :SHARE], ADD)
+        nc.vector.tensor_tensor(bb[:, SHARE:B_COLS], b_banks[0][:, SHARE:], f1[:, SHARE:B_COLS], ADD)
+        nc.vector.tensor_tensor(bb[:, B_COLS:], b_banks[1][:], f1[:, B_COLS:], ADD)
 
         w = keep.tile([P, I], F32, name="w")
         nc.scalar.activation(w[:], bb[:].indirect(l3[:]), COPY, scale=sb_col[:])
         nc.scalar.activation(f2[:].indirect(l4[:]), w[:], COPY)
 
         aa = keep.tile([P, T], F32, name="aa")
-        nc.vector.tensor_tensor(aa[:], a_sb[:], f2[:], SUB)
+        nc.gpsimd.tensor_tensor(aa[:, SPLIT:], a_sb[:, SPLIT:], f2[:, SPLIT:], SUB)
+        nc.vector.tensor_tensor(aa[:, :512], a_banks[0][:], f2[:, :512], SUB)
+        nc.vector.tensor_tensor(aa[:, 512:SPLIT], a_banks[1][:, : SPLIT - 512], f2[:, 512:SPLIT], SUB)
 
         for h in range(2):
             part = slice(h * LIST_COLS // 2, (h + 1) * LIST_COLS // 2)

from contextlib import ExitStack

import concourse.mybir as mybir

D, T, U, I, Q = 512, 1024, 1024, 512, 128
FLOPS = 2 * D * Q * (T + U)

F32 = mybir.dt.float32
BF16 = mybir.dt.bfloat16
I32 = mybir.dt.int32
U32 = mybir.dt.uint32
U16 = mybir.dt.uint16
U8 = mybir.dt.uint8
FP8X4 = mybir.dt.float8_e4m3fn_x4
FP4X4 = mybir.dt.float4_e2m1fn_x4
COPY = mybir.ActivationFunctionType.Copy
ADD = mybir.AluOpType.add
SUB = mybir.AluOpType.subtract

P = 128
PACK = 4
A_PIECES = (512, 256, 128, 128)
SHARE = 352
SPLIT = T - SHARE
C_LOADS = ((0, 512), (512, 768), (768, 1024))
B_COLS = 512
HALF = I // 2
LIST_COLS = I // 16


def tile_attend_scaledreturn_two_kernel(
    tc, query, cache_words, cache_scales, draft_words, draft_scales, sa, sb, offs, offs2, offs3, offs4, offs5, out
):
    nc = tc.nc
    with ExitStack() as ctx:
        keep = ctx.enter_context(tc.tile_pool(name="keep", bufs=1))
        psum = ctx.enter_context(tc.psum_pool(name="psum", bufs=1))

        def load_list(src, name):
            tile = keep.tile([P, LIST_COLS], U16, name=name)
            nc.sync.dma_start(tile[:], src)
            return tile

        def load_scales(engine, src, name):
            plane = keep.tile([P, T], U8, name=name, align_bytes=64)
            for quad in range(4):
                engine.dma_start(
                    plane[32 * quad : 32 * quad + 4, :].bitcast(I32),
                    src[0, 4 * quad : 4 * quad + 4, :].bitcast(I32),
                )
            return plane

        q_raw = keep.tile([P, PACK, Q], F32, name="q_raw")
        nc.sync.dma_start(q_raw[:], query.rearrange("(p j) q -> p j q", j=PACK))
        c_scales = load_scales(nc.sync, cache_scales, "c_scales")
        c_flat = cache_words[0].rearrange("p n t -> p (n t)")
        c_words = []
        for c0, c1 in C_LOADS:
            tile = keep.tile([P, c1 - c0], I32, name=f"c_words{c0}", align_bytes=64)
            nc.sync.dma_start(tile[:], c_flat[:, PACK * c0 : PACK * c1].bitcast(I32))
            c_words.append(tile)
        l1 = load_list(offs, "l1")
        l2 = load_list(offs2, "l2")
        d_words = keep.tile([P, 2 * U], U8, name="d_words", align_bytes=64)
        nc.sync.dma_start(d_words[:].bitcast(I32), draft_words[0].bitcast(I32))
        d_scales = load_scales(nc.sync, draft_scales, "d_scales")
        l3 = load_list(offs3, "l3")
        sb_col = keep.tile([P, 1], F32, name="sb_col")
        nc.sync.dma_start(sb_col[:], sb)
        l4 = load_list(offs4, "l4")
        l5 = load_list(offs5, "l5")
        sa_col = keep.tile([P, 1], F32, name="sa_col")
        nc.sync.dma_start(sa_col[:], sa)

        f1 = keep.tile([P, U], F32, name="f1")
        f2 = keep.tile([P, T], F32, name="f2")
        nc.vector.memset(f1[:], 0.0)
        nc.vector.memset(f2[:], 0.0)

        q_bf = keep.tile([P, Q, PACK], BF16, name="q_bf", align_bytes=64)
        nc.vector.tensor_copy(
            out=q_bf[:].rearrange("p (c i) t -> p c t i", i=4),
            in_=q_raw[:].rearrange("p t (c i) -> p c t i", i=4),
        )
        q_words = keep.tile([P, Q], U32, name="q_words", align_bytes=64)
        q_scales = keep.tile([P, Q], U8, name="q_scales", align_bytes=64)
        nc.vector.quantize_mx(
            out=q_words[:].bitcast(FP8X4), scales=q_scales[:], in_=q_bf[:].rearrange("p q t -> p (q t)")
        )

        a_sb = keep.tile([P, T], F32, name="a_sb")
        a_banks = []
        start = 0
        for c, width in enumerate(A_PIECES):
            bank = psum.tile([P, width], F32, name=f"a_bank{c}")
            cols = slice(start, start + width)
            h = max(n for n, load in enumerate(C_LOADS) if load[0] <= start)
            c0 = start - C_LOADS[h][0]
            nc.tensor.matmul_mx(
                out=bank[:],
                lhsT=q_words[:].bitcast(FP8X4),
                lhsT_scale=q_scales[:],
                rhs=c_words[h][:, c0 : c0 + width].bitcast(FP8X4),
                rhs_scale=c_scales[:, cols],
                start=True,
                stop=True,
            )
            if c in (0, 3):
                nc.scalar.copy(a_sb[:, cols], bank[:])
            else:
                nc.vector.tensor_copy(out=a_sb[:, cols], in_=bank[:])
            a_banks.append(bank)
            start = start + width

        b_banks = []
        for c in range(U // B_COLS):
            bank = psum.tile([P, B_COLS], F32, name=f"b_bank{c}")
            nc.tensor.matmul_mx(
                out=bank[:],
                lhsT=q_words[:].bitcast(FP8X4),
                lhsT_scale=q_scales[:],
                rhs=d_words[:, 2 * c * B_COLS : 2 * (c + 1) * B_COLS].bitcast(FP4X4),
                rhs_scale=d_scales[:, c * B_COLS : (c + 1) * B_COLS],
                start=True,
                stop=True,
            )
            b_banks.append(bank)

        picked = keep.tile([P, I], F32, name="picked")
        nc.scalar.activation(picked[:, :HALF], a_sb[:].indirect(l1[:, : LIST_COLS // 2]), COPY)
        nc.vector.tensor_copy(picked[:, HALF:], a_sb[:].indirect(l1[:, LIST_COLS // 2 :]))
        nc.scalar.activation(f1[:].indirect(l2[:]), picked[:], COPY)

        b_head = a_sb[:, :SHARE]
        nc.vector.tensor_copy(out=b_head, in_=b_banks[0][:, :SHARE])
        bb = keep.tile([P, U], F32, name="bb")
        nc.gpsimd.tensor_tensor(bb[:, :SHARE], b_head, f1[:, :SHARE], ADD)
        nc.vector.tensor_tensor(bb[:, SHARE:B_COLS], b_banks[0][:, SHARE:], f1[:, SHARE:B_COLS], ADD)
        nc.vector.tensor_tensor(bb[:, B_COLS:], b_banks[1][:], f1[:, B_COLS:], ADD)

        w = keep.tile([P, I], F32, name="w")
        nc.scalar.activation(w[:], bb[:].indirect(l3[:]), COPY, scale=sb_col[:])
        nc.scalar.activation(f2[:].indirect(l4[:]), w[:], COPY)

        aa = keep.tile([P, T], F32, name="aa")
        nc.gpsimd.tensor_tensor(aa[:, SPLIT:], a_sb[:, SPLIT:], f2[:, SPLIT:], SUB)
        nc.vector.tensor_tensor(aa[:, :512], a_banks[0][:], f2[:, :512], SUB)
        nc.vector.tensor_tensor(aa[:, 512:SPLIT], a_banks[1][:, : SPLIT - 512], f2[:, 512:SPLIT], SUB)

        for h in range(2):
            part = slice(h * LIST_COLS // 2, (h + 1) * LIST_COLS // 2)
            cols = slice(h * HALF, (h + 1) * HALF)
            v = keep.tile([P, HALF], F32, name=f"v{h}")
            nc.scalar.activation(v[:], aa[:].indirect(l5[:, part]), COPY, scale=sa_col[:])
            y = keep.tile([P, HALF], F32, name=f"y{h}")
            nc.vector.tensor_tensor(y[:], v[:], w[:, cols], SUB)
            nc.sync.dma_start(out[:, cols], y[:])
